import numpy as np
import ml_dtypes


def mxq(x, axis, fmt="e4m3"):
    dtype, down = {"e4m3": (ml_dtypes.float8_e4m3fn, 7), "e5m2": (ml_dtypes.float8_e5m2, 14)}[fmt]
    v = np.moveaxis(np.asarray(x, np.float32).astype(ml_dtypes.bfloat16).astype(np.float64), axis, -1)
    blocks = v.reshape(v.shape[:-1] + (-1, 32))
    amax = np.abs(blocks).max(-1, keepdims=True)
    byte = np.maximum(np.where(amax > 0, np.frexp(amax)[1] - 1 + 127, 0) - down, 1)
    scale = np.exp2(byte - 127.0)
    codes = (blocks / scale).astype(np.float32).astype(dtype).astype(np.float64)
    return np.moveaxis((codes * scale).reshape(v.shape), -1, axis)


WIDE = False


def mx_kscale(k):
    if not WIDE:
        return np.ones(k)
    levels = np.array([10, -10, 5, -5, 0])
    if k % 512:
        return np.exp2(np.random.permutation(np.resize(levels, k // 32))).repeat(32)
    a = np.empty((k // 512, 16))
    for p in range(k // 512):
        a[p, :8] = np.random.permutation(np.resize(levels, 8))
        for g in range(8):
            far = levels[np.abs(levels - a[p, g]) >= 10]
            a[p, g + 8] = far[np.random.randint(len(far))]
    return np.exp2(a.ravel()).repeat(32)


def f64(x):
    return np.asarray(x).astype(np.float64)


def striped(idx):
    return np.tile(np.asarray(idx).reshape(-1, 16).T, (8, 1)).astype(np.uint16)


def unstriped(offs):
    return offs[:16].T.reshape(-1).astype(np.int64)


def striped8(idx):
    return np.asarray(idx).reshape(8, -1, 16).transpose(0, 2, 1).reshape(128, -1).astype(np.uint16)


def unstriped8(offs):
    return offs.reshape(8, 16, -1).transpose(0, 2, 1).reshape(8, -1).astype(np.int64)


def pick8(x, idx, run):
    r = np.arange(len(x))
    return x[r[:, None], idx[r % (8 * run) // run]]


E2M1 = np.array([0.0, 0.5, 1.0, 1.5, 2.0, 3.0, 4.0, 6.0, -0.0, -0.5, -1.0, -1.5, -2.0, -3.0, -4.0, -6.0])


def pack_weight(w, fmt):
    k, n = w.shape
    w = f64(np.asarray(w, np.float32).astype(ml_dtypes.bfloat16)).reshape(k // 32, 32, n)
    amax = np.abs(w).max(1)
    if fmt == "e4m3":
        byte = np.frexp(amax)[1] - 1 + 127 - 7
    else:
        mant, ex = np.frexp(amax / 6.0)
        byte = np.where(mant > 0.5, ex, ex - 1) + 127
    byte = np.clip(np.where(amax > 0, byte, 1), 1, 254)
    scaled = (w * np.exp2(127.0 - byte)[:, None, :]).reshape(k, n).astype(np.float32)
    by_word = np.ascontiguousarray(scaled.reshape(k // 512, 128, 4, n).transpose(0, 1, 3, 2))
    if fmt == "e4m3":
        words = by_word.astype(ml_dtypes.float8_e4m3fn).view(np.uint8)
    else:
        c = by_word.astype(ml_dtypes.float4_e2m1fn).view(np.uint8) & 0xF
        words = (c[..., 0::2] | (c[..., 1::2] << 4)).reshape(k // 512, 128, 2 * n)
    return np.ascontiguousarray(words), np.ascontiguousarray(byte.astype(np.uint8).reshape(k // 512, 16, n))


def unpack_weight(words, scales, fmt):
    g, _, n = scales.shape
    words = np.ascontiguousarray(words).reshape(g, 128, n, -1)
    if fmt == "e4m3":
        vals = words.view(ml_dtypes.float8_e4m3fn).astype(np.float64)
    else:
        nib = np.empty((g, 128, n, 4), np.uint8)
        nib[..., 0::2] = words & 0xF
        nib[..., 1::2] = words >> 4
        vals = E2M1[nib]
    vals = vals * np.repeat(np.exp2(scales.astype(np.float64) - 127.0), 8, axis=1)[..., None]
    return vals.transpose(0, 1, 3, 2).reshape(g * 512, n)


K, J, R, T, F, C, N, S = 512, 384, 512, 1024, 1024, 512, 256, 1024


def setup_inputs():
    n = np.random.standard_normal
    idx = np.random.permutation(T)[:J]
    idx2 = np.random.permutation(F)[:R]
    idx3 = np.stack([np.random.permutation(C)[:J] for _ in range(8)])
    idx4 = np.stack([np.random.permutation(C)[:J] for _ in range(8)])
    idx5 = np.stack([np.random.permutation(C)[:J] for _ in range(8)])
    idx6 = np.random.permutation(S)[:N]
    fk = mx_kscale(K)
    fr = mx_kscale(R)
    tr = np.ones(F)
    tr[idx2] = fr
    xtp = pack_weight(n((K, T)) * fk[:, None], "e2m1")
    wtp = pack_weight(n((K, F)) * 1 / np.sqrt(K) / fk[:, None] * tr, "e4m3")
    vsp = pack_weight(n((R, S)) * 1 / np.sqrt(R) / fr[:, None], "e2m1")
    return {
        "xt_words": xtp[0],
        "xt_scales": xtp[1],
        "wt_words": wtp[0],
        "wt_scales": wtp[1],
        "vs_words": vsp[0],
        "vs_scales": vsp[1],
        "offs": striped(idx),
        "offs2": striped(idx2),
        "offs3": striped8(idx3),
        "offs4": striped8(idx4),
        "offs5": striped8(idx5),
        "offs6": striped(idx6),
    }


def reference(xt_words, xt_scales, wt_words, wt_scales, vs_words, vs_scales, offs, offs2, offs3, offs4, offs5, offs6):
    idx = unstriped(offs)
    idx2 = unstriped(offs2)
    idx3 = unstriped8(offs3)
    idx4 = unstriped8(offs4)
    idx5 = unstriped8(offs5)
    idx6 = unstriped(offs6)
    xtu = unpack_weight(xt_words, xt_scales, "e2m1")
    wtu = unpack_weight(wt_words, wt_scales, "e4m3")
    vsu = unpack_weight(vs_words, vs_scales, "e2m1")
    wtidx2g = wtu[:, idx2]
    xtidxg = xtu[:, idx]
    a = wtidx2g.T @ xtidxg
    pw = np.zeros((R, C))
    pw[np.arange(R)[:, None], idx3[np.arange(R) % 512 // 64]] = a
    pv = np.zeros((R, C))
    pv[np.arange(R)[:, None], idx4[np.arange(R) % 512 // 64]] = a
    pu = np.zeros((R, C))
    pu[np.arange(R)[:, None], idx5[np.arange(R) % 512 // 64]] = a
    hid = np.maximum(np.minimum(pw, pv), np.minimum(np.maximum(pw, pv), pu))
    vsidx6g = vsu[:, idx6]
    hidq = mxq(hid, 0, "e4m3")
    y = vsidx6g.T @ hidq
    return y

@@ -1,0 +1,189 @@
+from contextlib import ExitStack
+
+import concourse.mybir as mybir
+
+K, J, R, T, F, C, N, S = 512, 384, 512, 1024, 1024, 512, 256, 1024
+FLOPS = 2 * K * R * J + 2 * R * N * C
+
+F32 = mybir.dt.float32
+BF16 = mybir.dt.bfloat16
+I32 = mybir.dt.int32
+U32 = mybir.dt.uint32
+U16 = mybir.dt.uint16
+U8 = mybir.dt.uint8
+FP8X4 = mybir.dt.float8_e4m3fn_x4
+FP4X4 = mybir.dt.float4_e2m1fn_x4
+MIN = mybir.AluOpType.min
+MAX = mybir.AluOpType.max
+COPY = mybir.ActivationFunctionType.Copy
+
+P = 128
+PACK = 4
+STRIPE = 16
+J_FIRST = 128
+C_HALF = 256
+
+
+def tile_picked_tokens_store_one_medianboards_store_plain_kernel(
+    tc, xt_words, xt_scales, wt_words, wt_scales, vs_words, vs_scales, offs, offs2, offs3, offs4, offs5, offs6, out
+):
+    nc = tc.nc
+    with ExitStack() as ctx:
+        keep = ctx.enter_context(tc.tile_pool(name="keep", bufs=1))
+        psum = ctx.enter_context(tc.psum_pool(name="psum", bufs=1))
+
+        def sb(name, cols, dtype):
+            return keep.tile([P, cols], dtype, name=name, align_bytes=64)
+
+        def load_list(name, src):
+            tile = keep.tile(list(src.shape), U16, name=name)
+            nc.sync.dma_start(tile[:], src)
+            return tile
+
+        def zeroed_scale_window(name, cols):
+            tile = sb(name, cols, U8)
+            nc.vector.memset(tile[:].bitcast(I32), 0)
+            return tile
+
+        def load_scale_rows(tile, src):
+            for q in range(4):
+                nc.sync.dma_start(tile[32 * q : 32 * q + 4, :].bitcast(I32), src[0, 4 * q : 4 * q + 4, :].bitcast(I32))
+
+        ws_win = zeroed_scale_window("ws_win", F)
+        xs_win = zeroed_scale_window("xs_win", T)
+        vs_win = zeroed_scale_window("vs_win", S)
+        board_w = sb("board_w", C, F32)
+        board_v = sb("board_v", C, F32)
+        board_u = sb("board_u", C, F32)
+        for board in (board_w, board_v, board_u):
+            nc.vector.memset(board[:], 0.0)
+
+        list_f = load_list("list_f", offs2)
+        load_scale_rows(ws_win, wt_scales)
+        ww_win = sb("ww_win", F, U32)
+        nc.sync.dma_start(ww_win[:].bitcast(I32), wt_words[0].rearrange("p f b -> p (f b)").bitcast(I32))
+        list_t = load_list("list_t", offs)
+        list_w = load_list("list_w", offs3)
+        xw_win = sb("xw_win", T, U16)
+        nc.sync.dma_start(xw_win[:].bitcast(I32), xt_words[0].bitcast(I32))
+        load_scale_rows(xs_win, xt_scales)
+        list_v = load_list("list_v", offs4)
+        list_u = load_list("list_u", offs5)
+        list_s = load_list("list_s", offs6)
+        vw_win = sb("vw_win", S, U16)
+        nc.sync.dma_start(vw_win[:].bitcast(I32), vs_words[0].bitcast(I32))
+        load_scale_rows(vs_win, vs_scales)
+
+        w_scales = sb("w_scales", R, U8)
+        w_words = sb("w_words", R, U32)
+        nc.vector.tensor_copy(w_scales[:].rearrange("p (t m) -> p m t", t=PACK), ws_win[:].indirect(list_f[:]))
+        nc.vector.tensor_copy(w_words[:].rearrange("p (t m) -> p m t", t=PACK), ww_win[:].indirect(list_f[:]))
+
+        spans = [(0, J_FIRST), (J_FIRST, J)]
+        x_words, x_scales = [], []
+
+        def gather_tokens(i):
+            j0, j1 = spans[i]
+            words = keep.tile([P, 2 * (j1 - j0)], U8, name="x_words", align_bytes=64)
+            scales = sb("x_scales%d" % i, j1 - j0, U8)
+            entries = list_t[:, j0 // STRIPE : j1 // STRIPE]
+            nc.vector.tensor_copy(words[:].bitcast(U16), xw_win[:].indirect(entries))
+            nc.vector.tensor_copy(scales[:], xs_win[:].indirect(entries))
+            x_words.append(words)
+            x_scales.append(scales)
+
+        def first_product(acc, t, i):
+            cols = slice(P * t, P * (t + 1))
+            nc.tensor.matmul_mx(
+                out=acc,
+                lhsT=w_words[:, cols].bitcast(FP8X4),
+                lhsT_scale=w_scales[:, cols],
+                rhs=x_words[i][:].bitcast(FP4X4),
+                rhs_scale=x_scales[i][:],
+                start=True,
+                stop=True,
+            )
+
+        def scatter(board, entries, a, j0, j1):
+            nc.scalar.activation(board[:].indirect(entries[:, j0 // STRIPE : j1 // STRIPE]), a[:, j0:j1], COPY)
+
+        a_sb = [sb("a%d" % t, J, F32) for t in range(PACK)]
+
+        def bank():
+            return psum.tile([P, C], F32, name="bank", bufs=8)
+
+        boards = ((board_w, list_w), (board_v, list_v), (board_u, list_u))
+
+        gather_tokens(0)
+        acc_first = bank()
+        accs = [bank() for t in range(PACK)]
+        first_product(acc_first[:, :J_FIRST], 0, 0)
+        for t in range(1, PACK):
+            first_product(accs[t][:, :J_FIRST], t, 0)
+        nc.scalar.activation(a_sb[0][:, :J_FIRST], acc_first[:, :J_FIRST], COPY)
+        for board, entries in boards:
+            scatter(board, entries, a_sb[0], 0, J_FIRST)
+
+        gather_tokens(1)
+        for t in range(PACK):
+            j0 = J_FIRST if t == 0 else 0
+            first_product(accs[t][:, J_FIRST:J], t, 1)
+            nc.vector.tensor_copy(a_sb[t][:, j0:], accs[t][:, j0:J])
+
+        v_words = sb("v_words", 2 * N, U8)
+        v_scales = sb("v_scales", N, U8)
+        nc.vector.tensor_copy(v_words[:].bitcast(U16), vw_win[:].indirect(list_s[:]))
+        nc.vector.tensor_copy(v_scales[:], vs_win[:].indirect(list_s[:]))
+
+        low = sb("low", C, F32)
+        high = sb("high", C, F32)
+        capped = sb("capped", C, F32)
+        hid = sb("hid", PACK * C, BF16)
+        hid_slots = hid[:].rearrange("p (c t) -> p c t", t=PACK)
+        halves = [slice(0, C_HALF), slice(C_HALF, C)]
+
+        pair = keep.tile([P, 2, C_HALF], F32, name="pair")
+        left, right = halves
+
+        for t in range(PACK):
+            j0 = J_FIRST if t == 0 else 0
+            scatter(board_w, list_w, a_sb[t], j0, J)
+            scatter(board_v, list_v, a_sb[t], j0, J)
+            nc.vector.tensor_tensor(high[:], board_w[:], board_v[:], MAX)
+            nc.vector.tensor_tensor(low[:], board_w[:], board_v[:], MIN)
+            scatter(board_u, list_u, a_sb[t], j0, J)
+            if t < 2:
+                nc.vector.tensor_tensor(capped[:], high[:], board_u[:], MIN)
+                nc.vector.tensor_tensor(hid_slots[:, :, t], low[:], capped[:], MAX)
+            else:
+                for cols in halves:
+                    nc.vector.tensor_tensor(capped[:, cols], high[:, cols], board_u[:, cols], MIN)
+                nc.vector.tensor_tensor(pair[:, t - 2, :], low[:, left], capped[:, left], MAX)
+                nc.vector.tensor_tensor(hid_slots[:, right, t], low[:, right], capped[:, right], MAX)
+        nc.scalar.copy(hid_slots[:, left, 2:4], pair[:].rearrange("p t c -> p c t"))
+
+        for h, cols in enumerate(halves):
+            h_words = sb("h_words%d" % h, C_HALF, U32)
+            h_scales = sb("h_scales%d" % h, C_HALF, U8)
+            nc.vector.quantize_mx(
+                out=h_words[:].bitcast(FP8X4),
+                scales=h_scales[:],
+                in_=hid[:, PACK * cols.start : PACK * cols.stop],
+            )
+            for n in range(N // P):
+                y = bank()
+                nc.tensor.matmul_mx(
+                    out=y[:, :C_HALF],
+                    lhsT=v_words[:, 2 * P * n : 2 * P * (n + 1)].bitcast(FP4X4),
+                    lhsT_scale=v_scales[:, P * n : P * (n + 1)],
+                    rhs=h_words[:].bitcast(FP8X4),
+                    rhs_scale=h_scales[:],
+                    start=True,
+                    stop=True,
+                )
+                y_sb = sb("y_sb%d%d" % (h, n), C_HALF, F32)
+                if n == 1:
+                    nc.vector.tensor_copy(y_sb[:], y[:, :C_HALF])
+                else:
+                    nc.scalar.copy(y_sb[:], y[:, :C_HALF])
+                nc.sync.dma_start(out[P * n : P * (n + 1), cols], y_sb[:])

@@ -21,7 +21,7 @@ P = 128
 PACK = 4
 STRIPE = 16
 J_FIRST = 128
-C_HALF = 256
+C_CHUNK = 128
 
 
 def tile_picked_tokens_store_one_medianboards_store_plain_kernel(
@@ -140,10 +140,48 @@ def tile_picked_tokens_store_one_medianboards_store_plain_kernel(
         capped = sb("capped", C, F32)
         hid = sb("hid", PACK * C, BF16)
         hid_slots = hid[:].rearrange("p (c t) -> p c t", t=PACK)
-        halves = [slice(0, C_HALF), slice(C_HALF, C)]
+        chunks = [slice(C_CHUNK * c, C_CHUNK * (c + 1)) for c in range(C // C_CHUNK)]
+        inner = slice(chunks[1].start, chunks[2].stop)
+        pair = keep.tile([P, 2, C], F32, name="pair")
 
-        pair = keep.tile([P, 2, C_HALF], F32, name="pair")
-        left, right = halves
+        def cap(cols):
+            nc.vector.tensor_tensor(capped[:, cols], high[:, cols], board_u[:, cols], MIN)
+
+        def median(dst, cols):
+            nc.vector.tensor_tensor(dst, low[:, cols], capped[:, cols], MAX)
+
+        def place_pair(cols):
+            nc.scalar.copy(hid_slots[:, cols, 2:4], pair[:, :, cols].rearrange("p t c -> p c t"))
+
+        h_words = [sb("h_words%d" % c, C_CHUNK, U32) for c in range(len(chunks))]
+        h_scales = [sb("h_scales%d" % c, C_CHUNK, U8) for c in range(len(chunks))]
+        out_rows = out.rearrange("(a p) c -> p a c", p=P)
+
+        def quantise(c):
+            nc.vector.quantize_mx(
+                out=h_words[c][:].bitcast(FP8X4),
+                scales=h_scales[c][:],
+                in_=hid[:, PACK * chunks[c].start : PACK * chunks[c].stop],
+            )
+
+        def second_product(acc, n, c):
+            nc.tensor.matmul_mx(
+                out=acc,
+                lhsT=v_words[:, 2 * P * n : 2 * P * (n + 1)].bitcast(FP4X4),
+                lhsT_scale=v_scales[:, P * n : P * (n + 1)],
+                rhs=h_words[c][:].bitcast(FP8X4),
+                rhs_scale=h_scales[c][:],
+                start=True,
+                stop=True,
+            )
+
+        def finish(c):
+            y = bank()
+            y_sb = sb("y_sb%d" % c, 2 * C_CHUNK, F32)
+            for n in range(2):
+                second_product(y[:, C_CHUNK * n : C_CHUNK * (n + 1)], n, c)
+            nc.scalar.copy(y_sb[:], y[:, : 2 * C_CHUNK])
+            nc.sync.dma_start(out_rows[:, :, chunks[c]], y_sb[:].rearrange("p (a c) -> p a c", a=2))
 
         for t in range(PACK):
             j0 = J_FIRST if t == 0 else 0
@@ -153,37 +191,34 @@ def tile_picked_tokens_store_one_medianboards_store_plain_kernel(
             nc.vector.tensor_tensor(low[:], board_w[:], board_v[:], MIN)
             scatter(board_u, list_u, a_sb[t], j0, J)
             if t < 2:
-                nc.vector.tensor_tensor(capped[:], high[:], board_u[:], MIN)
-                nc.vector.tensor_tensor(hid_slots[:, :, t], low[:], capped[:], MAX)
-            else:
-                for cols in halves:
-                    nc.vector.tensor_tensor(capped[:, cols], high[:, cols], board_u[:, cols], MIN)
-                nc.vector.tensor_tensor(pair[:, t - 2, :], low[:, left], capped[:, left], MAX)
-                nc.vector.tensor_tensor(hid_slots[:, right, t], low[:, right], capped[:, right], MAX)
-        nc.scalar.copy(hid_slots[:, left, 2:4], pair[:].rearrange("p t c -> p c t"))
+                cap(slice(0, C))
+                median(hid_slots[:, :, t], slice(0, C))
+            elif t == 2:
+                cap(slice(0, C))
+                median(pair[:, 0, inner], inner)
+                median(hid_slots[:, chunks[0], t], chunks[0])
+                median(hid_slots[:, chunks[3], t], chunks[3])
 
-        for h, cols in enumerate(halves):
-            h_words = sb("h_words%d" % h, C_HALF, U32)
-            h_scales = sb("h_scales%d" % h, C_HALF, U8)
-            nc.vector.quantize_mx(
-                out=h_words[:].bitcast(FP8X4),
-                scales=h_scales[:],
-                in_=hid[:, PACK * cols.start : PACK * cols.stop],
-            )
-            for n in range(N // P):
-                y = bank()
-                nc.tensor.matmul_mx(
-                    out=y[:, :C_HALF],
-                    lhsT=v_words[:, 2 * P * n : 2 * P * (n + 1)].bitcast(FP4X4),
-                    lhsT_scale=v_scales[:, P * n : P * (n + 1)],
-                    rhs=h_words[:].bitcast(FP8X4),
-                    rhs_scale=h_scales[:],
-                    start=True,
-                    stop=True,
-                )
-                y_sb = sb("y_sb%d%d" % (h, n), C_HALF, F32)
-                if n == 1:
-                    nc.vector.tensor_copy(y_sb[:], y[:, :C_HALF])
-                else:
-                    nc.scalar.copy(y_sb[:], y[:, :C_HALF])
-                nc.sync.dma_start(out[P * n : P * (n + 1), cols], y_sb[:])
+        t = PACK - 1
+        cap(chunks[0])
+        cap(chunks[1])
+        median(hid_slots[:, chunks[0], t], chunks[0])
+        median(pair[:, 1, chunks[1]], chunks[1])
+        place_pair(chunks[1])
+        cap(slice(chunks[2].start, C))
+        quantise(0)
+        median(pair[:, 1, chunks[2]], chunks[2])
+        place_pair(chunks[2])
+        finish(0)
+        quantise(1)
+        finish(1)
+        median(hid_slots[:, chunks[3], t], chunks[3])
+        quantise(2)
+        finish(2)
+        quantise(3)
+        y_sb = sb("y_last", 2 * C_CHUNK, F32)
+        for n, copy in enumerate((nc.vector.tensor_copy, nc.scalar.copy)):
+            y = bank()
+            second_product(y[:, :C_CHUNK], n, 3)
+            copy(y_sb[:, C_CHUNK * n : C_CHUNK * (n + 1)], y[:, :C_CHUNK])
+        nc.sync.dma_start(out_rows[:, :, chunks[3]], y_sb[:].rearrange("p (a c) -> p a c", a=2))

from contextlib import ExitStack

import concourse.mybir as mybir

K, J, R, T, F, C, N, S = 512, 384, 512, 1024, 1024, 512, 256, 1024
FLOPS = 2 * K * R * J + 2 * R * N * C

F32 = mybir.dt.float32
BF16 = mybir.dt.bfloat16
I32 = mybir.dt.int32
U32 = mybir.dt.uint32
U16 = mybir.dt.uint16
U8 = mybir.dt.uint8
FP8X4 = mybir.dt.float8_e4m3fn_x4
FP4X4 = mybir.dt.float4_e2m1fn_x4
MIN = mybir.AluOpType.min
MAX = mybir.AluOpType.max
COPY = mybir.ActivationFunctionType.Copy

P = 128
PACK = 4
STRIPE = 16
J_FIRST = 128
C_CHUNK = 128


def tile_picked_tokens_store_one_medianboards_store_plain_kernel(
    tc, xt_words, xt_scales, wt_words, wt_scales, vs_words, vs_scales, offs, offs2, offs3, offs4, offs5, offs6, out
):
    nc = tc.nc
    with ExitStack() as ctx:
        keep = ctx.enter_context(tc.tile_pool(name="keep", bufs=1))
        psum = ctx.enter_context(tc.psum_pool(name="psum", bufs=1))

        def sb(name, cols, dtype):
            return keep.tile([P, cols], dtype, name=name, align_bytes=64)

        def load_list(name, src):
            tile = keep.tile(list(src.shape), U16, name=name)
            nc.sync.dma_start(tile[:], src)
            return tile

        def zeroed_scale_window(name, cols):
            tile = sb(name, cols, U8)
            nc.vector.memset(tile[:].bitcast(I32), 0)
            return tile

        def load_scale_rows(tile, src):
            for q in range(4):
                nc.sync.dma_start(tile[32 * q : 32 * q + 4, :].bitcast(I32), src[0, 4 * q : 4 * q + 4, :].bitcast(I32))

        ws_win = zeroed_scale_window("ws_win", F)
        xs_win = zeroed_scale_window("xs_win", T)
        vs_win = zeroed_scale_window("vs_win", S)
        board_w = sb("board_w", C, F32)
        board_v = sb("board_v", C, F32)
        board_u = sb("board_u", C, F32)
        for board in (board_w, board_v, board_u):
            nc.vector.memset(board[:], 0.0)

        list_f = load_list("list_f", offs2)
        load_scale_rows(ws_win, wt_scales)
        ww_win = sb("ww_win", F, U32)
        nc.sync.dma_start(ww_win[:].bitcast(I32), wt_words[0].rearrange("p f b -> p (f b)").bitcast(I32))
        list_t = load_list("list_t", offs)
        list_w = load_list("list_w", offs3)
        xw_win = sb("xw_win", T, U16)
        nc.sync.dma_start(xw_win[:].bitcast(I32), xt_words[0].bitcast(I32))
        load_scale_rows(xs_win, xt_scales)
        list_v = load_list("list_v", offs4)
        list_u = load_list("list_u", offs5)
        list_s = load_list("list_s", offs6)
        vw_win = sb("vw_win", S, U16)
        nc.sync.dma_start(vw_win[:].bitcast(I32), vs_words[0].bitcast(I32))
        load_scale_rows(vs_win, vs_scales)

        w_scales = sb("w_scales", R, U8)
        w_words = sb("w_words", R, U32)
        nc.vector.tensor_copy(w_scales[:].rearrange("p (t m) -> p m t", t=PACK), ws_win[:].indirect(list_f[:]))
        nc.vector.tensor_copy(w_words[:].rearrange("p (t m) -> p m t", t=PACK), ww_win[:].indirect(list_f[:]))

        spans = [(0, J_FIRST), (J_FIRST, J)]
        x_words, x_scales = [], []

        def gather_tokens(i):
            j0, j1 = spans[i]
            words = keep.tile([P, 2 * (j1 - j0)], U8, name="x_words", align_bytes=64)
            scales = sb("x_scales%d" % i, j1 - j0, U8)
            entries = list_t[:, j0 // STRIPE : j1 // STRIPE]
            nc.vector.tensor_copy(words[:].bitcast(U16), xw_win[:].indirect(entries))
            nc.vector.tensor_copy(scales[:], xs_win[:].indirect(entries))
            x_words.append(words)
            x_scales.append(scales)

        def first_product(acc, t, i):
            cols = slice(P * t, P * (t + 1))
            nc.tensor.matmul_mx(
                out=acc,
                lhsT=w_words[:, cols].bitcast(FP8X4),
                lhsT_scale=w_scales[:, cols],
                rhs=x_words[i][:].bitcast(FP4X4),
                rhs_scale=x_scales[i][:],
                start=True,
                stop=True,
            )

        def scatter(board, entries, a, j0, j1):
            nc.scalar.activation(board[:].indirect(entries[:, j0 // STRIPE : j1 // STRIPE]), a[:, j0:j1], COPY)

        a_sb = [sb("a%d" % t, J, F32) for t in range(PACK)]

        def bank():
            return psum.tile([P, C], F32, name="bank", bufs=8)

        boards = ((board_w, list_w), (board_v, list_v), (board_u, list_u))

        gather_tokens(0)
        acc_first = bank()
        accs = [bank() for t in range(PACK)]
        first_product(acc_first[:, :J_FIRST], 0, 0)
        for t in range(1, PACK):
            first_product(accs[t][:, :J_FIRST], t, 0)
        nc.scalar.activation(a_sb[0][:, :J_FIRST], acc_first[:, :J_FIRST], COPY)
        for board, entries in boards:
            scatter(board, entries, a_sb[0], 0, J_FIRST)

        gather_tokens(1)
        for t in range(PACK):
            j0 = J_FIRST if t == 0 else 0
            first_product(accs[t][:, J_FIRST:J], t, 1)
            nc.vector.tensor_copy(a_sb[t][:, j0:], accs[t][:, j0:J])

        v_words = sb("v_words", 2 * N, U8)
        v_scales = sb("v_scales", N, U8)
        nc.vector.tensor_copy(v_words[:].bitcast(U16), vw_win[:].indirect(list_s[:]))
        nc.vector.tensor_copy(v_scales[:], vs_win[:].indirect(list_s[:]))

        low = sb("low", C, F32)
        high = sb("high", C, F32)
        capped = sb("capped", C, F32)
        hid = sb("hid", PACK * C, BF16)
        hid_slots = hid[:].rearrange("p (c t) -> p c t", t=PACK)
        chunks = [slice(C_CHUNK * c, C_CHUNK * (c + 1)) for c in range(C // C_CHUNK)]
        inner = slice(chunks[1].start, chunks[2].stop)
        pair = keep.tile([P, 2, C], F32, name="pair")

        def cap(cols):
            nc.vector.tensor_tensor(capped[:, cols], high[:, cols], board_u[:, cols], MIN)

        def median(dst, cols):
            nc.vector.tensor_tensor(dst, low[:, cols], capped[:, cols], MAX)

        def place_pair(cols):
            nc.scalar.copy(hid_slots[:, cols, 2:4], pair[:, :, cols].rearrange("p t c -> p c t"))

        h_words = [sb("h_words%d" % c, C_CHUNK, U32) for c in range(len(chunks))]
        h_scales = [sb("h_scales%d" % c, C_CHUNK, U8) for c in range(len(chunks))]
        out_rows = out.rearrange("(a p) c -> p a c", p=P)

        def quantise(c):
            nc.vector.quantize_mx(
                out=h_words[c][:].bitcast(FP8X4),
                scales=h_scales[c][:],
                in_=hid[:, PACK * chunks[c].start : PACK * chunks[c].stop],
            )

        def second_product(acc, n, c):
            nc.tensor.matmul_mx(
                out=acc,
                lhsT=v_words[:, 2 * P * n : 2 * P * (n + 1)].bitcast(FP4X4),
                lhsT_scale=v_scales[:, P * n : P * (n + 1)],
                rhs=h_words[c][:].bitcast(FP8X4),
                rhs_scale=h_scales[c][:],
                start=True,
                stop=True,
            )

        def finish(c):
            y = bank()
            y_sb = sb("y_sb%d" % c, 2 * C_CHUNK, F32)
            for n in range(2):
                second_product(y[:, C_CHUNK * n : C_CHUNK * (n + 1)], n, c)
            nc.scalar.copy(y_sb[:], y[:, : 2 * C_CHUNK])
            nc.sync.dma_start(out_rows[:, :, chunks[c]], y_sb[:].rearrange("p (a c) -> p a c", a=2))

        for t in range(PACK):
            j0 = J_FIRST if t == 0 else 0
            scatter(board_w, list_w, a_sb[t], j0, J)
            scatter(board_v, list_v, a_sb[t], j0, J)
            nc.vector.tensor_tensor(high[:], board_w[:], board_v[:], MAX)
            nc.vector.tensor_tensor(low[:], board_w[:], board_v[:], MIN)
            scatter(board_u, list_u, a_sb[t], j0, J)
            if t < 2:
                cap(slice(0, C))
                median(hid_slots[:, :, t], slice(0, C))
            elif t == 2:
                cap(slice(0, C))
                median(pair[:, 0, inner], inner)
                median(hid_slots[:, chunks[0], t], chunks[0])
                median(hid_slots[:, chunks[3], t], chunks[3])

        t = PACK - 1
        cap(chunks[0])
        cap(chunks[1])
        median(hid_slots[:, chunks[0], t], chunks[0])
        median(pair[:, 1, chunks[1]], chunks[1])
        place_pair(chunks[1])
        cap(slice(chunks[2].start, C))
        quantise(0)
        median(pair[:, 1, chunks[2]], chunks[2])
        place_pair(chunks[2])
        finish(0)
        quantise(1)
        finish(1)
        median(hid_slots[:, chunks[3], t], chunks[3])
        quantise(2)
        finish(2)
        quantise(3)
        y_sb = sb("y_last", 2 * C_CHUNK, F32)
        for n, copy in enumerate((nc.vector.tensor_copy, nc.scalar.copy)):
            y = bank()
            second_product(y[:, :C_CHUNK], n, 3)
            copy(y_sb[:, C_CHUNK * n : C_CHUNK * (n + 1)], y[:, :C_CHUNK])
        nc.sync.dma_start(out_rows[:, :, chunks[3]], y_sb[:].rearrange("p (a c) -> p a c", a=2))
